import numpy as np
import ml_dtypes


def mxq(x, axis, fmt="e4m3"):
    dtype, down = {"e4m3": (ml_dtypes.float8_e4m3fn, 7), "e5m2": (ml_dtypes.float8_e5m2, 14)}[fmt]
    v = np.moveaxis(np.asarray(x, np.float32).astype(ml_dtypes.bfloat16).astype(np.float64), axis, -1)
    blocks = v.reshape(v.shape[:-1] + (-1, 32))
    amax = np.abs(blocks).max(-1, keepdims=True)
    byte = np.maximum(np.where(amax > 0, np.frexp(amax)[1] - 1 + 127, 0) - down, 1)
    scale = np.exp2(byte - 127.0)
    codes = (blocks / scale).astype(np.float32).astype(dtype).astype(np.float64)
    return np.moveaxis((codes * scale).reshape(v.shape), -1, axis)


WIDE = False


def mx_kscale(k):
    if not WIDE:
        return np.ones(k)
    levels = np.array([10, -10, 5, -5, 0])
    if k % 512:
        return np.exp2(np.random.permutation(np.resize(levels, k // 32))).repeat(32)
    a = np.empty((k // 512, 16))
    for p in range(k // 512):
        a[p, :8] = np.random.permutation(np.resize(levels, 8))
        for g in range(8):
            far = levels[np.abs(levels - a[p, g]) >= 10]
            a[p, g + 8] = far[np.random.randint(len(far))]
    return np.exp2(a.ravel()).repeat(32)


def f64(x):
    return np.asarray(x).astype(np.float64)


def striped(idx):
    return np.tile(idx.reshape(-1, 16).T, (8, 1)).astype(np.uint16)


def unstriped(offs):
    return offs[:16].T.reshape(-1).astype(np.int64)


def pack_weight(w):
    k, n = w.shape
    w = f64(np.asarray(w, np.float32).astype(ml_dtypes.bfloat16)).reshape(k // 32, 32, n)
    amax = np.abs(w).max(1)
    byte = np.clip(np.where(amax > 0, np.frexp(amax)[1] - 1 + 127 - 7, 1), 1, 254)
    scaled = (w * np.exp2(127.0 - byte)[:, None, :]).reshape(k, n).astype(np.float32)
    words = np.ascontiguousarray(scaled.reshape(k // 512, 128, 4, n).transpose(0, 1, 3, 2)).astype(ml_dtypes.float8_e4m3fn).view(np.uint8)
    return words, np.ascontiguousarray(byte.astype(np.uint8).reshape(k // 512, 16, n))


def unpack_weight(words, scales):
    g, p, n, _ = words.shape
    vals = np.ascontiguousarray(words).view(ml_dtypes.float8_e4m3fn).astype(np.float64) * np.repeat(np.exp2(scales.astype(np.float64) - 127.0), 8, axis=1)[..., None]
    return vals.transpose(0, 1, 3, 2).reshape(g * 512, n)


def sigmoid(v):
    return 1.0 / (1.0 + np.exp(-np.maximum(v, -700.0)))


K, T, S, V = 512, 1024, 512, 512
P = 2 ** 7


def setup_inputs():
    n = np.random.standard_normal
    s = mx_kscale(K)[:, None]
    packed_xT = pack_weight(n((K, T)) * s)
    packed_eT = pack_weight(n((K, T)) * s)
    return {
        "x_words": packed_xT[0],
        "x_scales": packed_xT[1],
        "hT": (n((K, V)) / np.sqrt(K) / s).astype(np.float32),
        "e_words": packed_eT[0],
        "e_scales": packed_eT[1],
        "lib": (np.random.uniform(200.0, 800.0, (V, 1))).astype(np.float32),
        "theta": (np.tile(np.random.uniform(0.5, 3.0, T), (P, 1))).astype(np.float32),
        "cnt": (np.floor(np.random.uniform(0.0, 1.0, (V, S)) ** 3 * 6)).astype(np.float32),
        "zero": ((np.random.uniform(size=(V, S)) < 0.4) * 1.0).astype(np.float32),
        "offs": striped(np.random.permutation(T)[:S]),
    }


def reference(x_words, x_scales, hT, e_words, e_scales, lib, theta, cnt, zero, offs):
    hTq = mxq(f64(hT), 0, "e4m3")
    xq = unpack_weight(x_words, x_scales)[:, unstriped(offs)]
    y = hTq.T @ xq
    ex = np.exp(y - y.max(axis=1, keepdims=True))
    mu = f64(lib) * (ex / ex.sum(axis=1, keepdims=True))
    lt = np.log(f64(theta)[:1][:, unstriped(offs)]) - (np.log(f64(theta)[:1][:, unstriped(offs)] + mu))
    nb1 = lt * (f64(theta)[:1][:, unstriped(offs)]) + f64(cnt) * (np.log(mu + 0.001) - (np.log(f64(theta)[:1][:, unstriped(offs)] + mu)))
    e_offs = unpack_weight(e_words, e_scales)[:, unstriped(offs)]
    pi = hTq.T @ e_offs
    sg = sigmoid(pi)
    l1 = nb1 + np.log(-1.0 * sg + 1.0001)
    l0 = np.log(sg + (np.exp(lt * (f64(theta)[:1][:, unstriped(offs)]))) * (-1.0 * sg + 1.0))
    return np.tanh(0.2 * (l1 + f64(zero) * (l0 - l1)))

@@ -1,0 +1,235 @@
+import math
+from contextlib import ExitStack
+
+import concourse.mybir as mybir
+from concourse.masks import make_identity
+
+K, T, S, V = 512, 1024, 512, 512
+FLOPS = 2 * 2 * K * V * S
+
+F32 = mybir.dt.float32
+BF16 = mybir.dt.bfloat16
+I32 = mybir.dt.int32
+U32 = mybir.dt.uint32
+U16 = mybir.dt.uint16
+U8 = mybir.dt.uint8
+FP8X4 = mybir.dt.float8_e4m3fn_x4
+ALU = mybir.AluOpType
+ACT = mybir.ActivationFunctionType
+AX = mybir.AxisListType
+
+P = 128
+PACK = 4
+NB = 4
+LOG_GAIN = 2.0 ** 12
+LOG_FLOOR = 2.0 ** -64
+
+
+def tile_picked_yzinb_sq_p_kernel(
+    tc, x_words, x_scales, hT, e_words, e_scales, lib, theta, cnt, zero, offs, out
+):
+    nc = tc.nc
+    blk = lambda b: slice(b * P, (b + 1) * P)
+
+    with ExitStack() as ctx:
+        sb = ctx.enter_context(tc.tile_pool(name="sb", bufs=1))
+        ps = ctx.enter_context(tc.psum_pool(name="ps", bufs=1))
+
+        def tiles(name, shape, dtype, n=NB):
+            return [sb.tile(shape, dtype, name=name + str(b), align_bytes=64) for b in range(n)]
+
+        def one(name, shape, dtype):
+            return sb.tile(shape, dtype, name=name, align_bytes=64)
+
+        offsets = sb.tile([P, S // 16], U16, name="offsets")
+        bank_a = [ps.tile([P, S], F32, name="bank_a" + str(b)) for b in range(NB)]
+        bank_b = [ps.tile([P, S], F32, name="bank_b" + str(b)) for b in range(NB)]
+
+        e_scale_table = one("e_scale_table", [P, T], U8)
+        x_scale_table = one("x_scale_table", [P, T], U8)
+        e_word_table = one("e_word_table", [P, T], U32)
+        x_word_table = one("x_word_table", [P, T], U32)
+        theta_table = one("theta_table", [P, T], F32)
+        h_raw = tiles("h_raw", [P, PACK, 2 * P], F32, 2)
+        cnt_sb = tiles("cnt_sb", [P, 2, S], F32, 2)
+        zero_sb = tiles("zero_sb", [P, 2, S], F32, 2)
+        lib_sb = one("lib_sb", [P, NB], F32)
+        ident = one("ident", [P, P], F32)
+
+        def load_scales(table, scales):
+            for q in range(4):
+                rows = scales[0, 4 * q : 4 * q + 4, :].bitcast(I32)
+                nc.sync.dma_start(
+                    out=table[32 * q : 32 * q + 32, :].bitcast(I32),
+                    in_=rows.partition_broadcast(8),
+                )
+
+        def load_words(table, words):
+            nc.sync.dma_start(out=table[:].bitcast(I32), in_=words[0].rearrange("p n t -> p (n t)").bitcast(I32))
+
+        def load_h(half):
+            cols = hT[:, half * 2 * P : (half + 1) * 2 * P]
+            nc.sync.dma_start(out=h_raw[half][:], in_=cols.rearrange("(p t) c -> p t c", t=PACK))
+
+        def load_rows(dst, src, half):
+            rows = src[half * 2 * P : (half + 1) * 2 * P, :]
+            nc.sync.dma_start(out=dst[half][:], in_=rows.rearrange("(i p) g -> p i g", p=P))
+
+        nc.gpsimd.memset(theta_table[:], 0.0)
+        nc.scalar.dma_start(out=theta_table[0:1, :], in_=theta[0:1, :])
+        make_identity(nc, ident[:])
+
+        nc.sync.dma_start(offsets[:], offs)
+        load_scales(e_scale_table, e_scales)
+        load_h(0)
+        load_words(e_word_table, e_words)
+        load_scales(x_scale_table, x_scales)
+        load_h(1)
+        load_words(x_word_table, x_words)
+        for half in range(2):
+            load_rows(zero_sb, zero, half)
+            load_rows(cnt_sb, cnt, half)
+        with nc.allow_non_contiguous_dma(reason="one library size a partition"):
+            nc.sync.dma_start(out=lib_sb[:], in_=lib.rearrange("(i p) o -> p (i o)", p=P))
+
+        def gather(name, table, dtype):
+            picked = one(name, [P, S], dtype)
+            nc.vector.tensor_copy(picked[:], table[:].indirect(offsets[:]))
+            return picked
+
+        h_bf = tiles("h_bf", [P, P, PACK], BF16)
+        h_codes = tiles("h_codes", [P, P], U32)
+        h_scales = tiles("h_scales", [P, P], U8)
+
+        def interleave(i):
+            src = h_raw[i // 2][:, :, blk(i % 2)]
+            nc.scalar.activation(
+                out=h_bf[i][:].rearrange("p (c n) t -> p c t n", n=4),
+                in_=src.rearrange("p t (c n) -> p c t n", n=4),
+                func=ACT.Copy,
+            )
+
+        def quantize(i):
+            nc.vector.quantize_mx(
+                out=h_codes[i][:].bitcast(FP8X4),
+                scales=h_scales[i][:],
+                in_=h_bf[i][:].rearrange("p c t -> p (c t)"),
+            )
+
+        def product(bank, i, codes, scales):
+            nc.tensor.matmul_mx(
+                out=bank[:],
+                lhsT=h_codes[i][:].bitcast(FP8X4),
+                lhsT_scale=h_scales[i][:],
+                rhs=codes[:].bitcast(FP8X4),
+                rhs_scale=scales[:],
+                start=True,
+                stop=True,
+            )
+
+        def turn(dst, src, start=True, stop=True):
+            nc.tensor.matmul(dst, src, ident[:], start=start, stop=stop, is_transpose=True)
+
+        for i in range(NB):
+            interleave(i)
+        e_scale = gather("e_scale", e_scale_table, U8)
+        theta_row = gather("theta_row", theta_table, F32)
+        quantize(0)
+        quantize(1)
+        e_code = gather("e_code", e_word_table, U32)
+        x_scale = gather("x_scale", x_scale_table, U8)
+        quantize(2)
+        quantize(3)
+        x_code = gather("x_code", x_word_table, U32)
+
+        th = one("th", [P, NB], F32)
+        inv_th = one("inv_th", [P, NB], F32)
+        eps_th = one("eps_th", [P, NB], F32)
+        for j in range(NB):
+            turn(bank_a[3][:, blk(j)], theta_row[:, blk(j)])
+        nc.vector.tensor_copy(th[:], bank_a[3][:, 0:S:P])
+        nc.vector.reciprocal(inv_th[:], th[:])
+        nc.vector.tensor_scalar(eps_th[:], inv_th[:], 0.001, None, ALU.mult)
+
+        tanh_half = one("tanh_half", [P, NB, S], F32)
+        for i in range(NB):
+            product(bank_b[i], i, e_code, e_scale)
+            nc.scalar.activation(out=tanh_half[:, i, :], in_=bank_b[i][:], func=ACT.Tanh, scale=0.5)
+
+        neg_max = one("neg_max", [P, NB], F32)
+        total = one("total", [P, NB], F32)
+        inv_total = one("inv_total", [P, NB], F32)
+        ex = tiles("ex", [P, S], F32)
+        mu = tiles("mu", [P, S], F32)
+        for i in range(NB):
+            product(bank_a[i], i, x_code, x_scale)
+            nc.vector.tensor_reduce(neg_max[:, i : i + 1], bank_a[i][:], AX.X, ALU.max, negate=True)
+            nc.scalar.activation(
+                out=ex[i][:], in_=bank_a[i][:], func=ACT.Exp, bias=neg_max[:, i : i + 1], accum_out=total[:, i : i + 1]
+            )
+        for i in range(NB):
+            nc.vector.reciprocal(inv_total[:, i : i + 1], total[:, i : i + 1])
+            nc.vector.tensor_scalar(
+                mu[i][:], ex[i][:], inv_total[:, i : i + 1], lib_sb[:, i : i + 1], ALU.mult, ALU.mult
+            )
+            for j in range(NB):
+                turn(bank_b[j][:, blk(i)], mu[i][:, blk(j)])
+
+        neg_cz = tiles("neg_cz", [P, S], F32)
+        for i in range(NB):
+            nc.vector.scalar_tensor_tensor(
+                neg_cz[i][:], zero_sb[i // 2][:, i % 2, :], 1.0, cnt_sb[i // 2][:, i % 2, :], ALU.subtract, ALU.mult
+            )
+            for j in range(NB):
+                turn(bank_a[j][:, blk(i)], neg_cz[i][:, blk(j)])
+
+        log_m = tiles("log_m", [P, V], F32)
+        log_l = tiles("log_l", [P, V], F32)
+        term_m = tiles("term_m", [P, V], F32)
+        term_l = tiles("term_l", [P, V], F32)
+        for j in range(NB):
+            col = slice(j, j + 1)
+            nc.scalar.activation(
+                out=log_m[j][:], in_=bank_b[j][:], func=ACT.Ln, scale=inv_th[:, col], bias=eps_th[:, col]
+            )
+            nc.scalar.activation(out=log_l[j][:], in_=bank_b[j][:], func=ACT.Ln, scale=inv_th[:, col], bias=1.0)
+            nc.vector.scalar_tensor_tensor(term_m[j][:], bank_a[j][:], -1.0, log_m[j][:], ALU.mult, ALU.mult)
+            nc.vector.scalar_tensor_tensor(
+                term_l[j][:], bank_a[j][:], th[:, col], log_l[j][:], ALU.subtract, ALU.mult
+            )
+            for i in range(NB):
+                turn(bank_b[j][:, blk(i)], term_m[j][:, blk(i)], start=(i == 0), stop=False)
+            for i in range(NB):
+                turn(bank_b[j][:, blk(i)], term_l[j][:, blk(i)], start=False, stop=(i == NB - 1))
+
+        keep = one("keep", [P, NB, S], F32)
+        drop = tiles("drop", [P, S], F32)
+        for i in range(NB):
+            z = zero_sb[i // 2][:, i % 2, :]
+            nc.vector.scalar_tensor_tensor(keep[:, i, :], z, -2e-4, tanh_half[:, i, :], ALU.mult, ALU.subtract)
+        for i in range(NB):
+            z = zero_sb[i // 2][:, i % 2, :]
+            nc.vector.scalar_tensor_tensor(drop[i][:], tanh_half[:, i, :], 1.0, z, ALU.add, ALU.mult)
+            for j in range(NB):
+                turn(bank_a[i][:, blk(j)], drop[i][:, blk(j)], start=(j == 0), stop=False)
+
+        nb = tiles("nb", [P, NB, P], F32)
+        kept = tiles("kept", [P, NB, P], F32)
+        for j in range(NB):
+            nc.scalar.activation(out=nb[j][:].rearrange("p i c -> p (i c)"), in_=bank_b[j][:], func=ACT.Exp)
+            nc.vector.scalar_tensor_tensor(kept[j][:], keep[:, :, blk(j)], 1.0002, nb[j][:], ALU.add, ALU.mult)
+            for i in range(NB):
+                turn(bank_a[i][:, blk(j)], kept[j][:, i, :], start=False, stop=(j == NB - 1))
+
+        log_w = tiles("log_w", [P, S], F32)
+        for i in range(NB):
+            nc.scalar.activation(out=log_w[i][:], in_=bank_a[i][:], func=ACT.Ln, scale=LOG_GAIN, bias=LOG_FLOOR)
+            for j in range(NB):
+                turn(bank_b[i][:, blk(j)], log_w[i][:, blk(j)])
+
+        result = tiles("result", [P, S], F32)
+        for i in range(NB):
+            nc.scalar.activation(
+                out=result[i][:], in_=bank_b[i][:], func=ACT.Tanh, scale=0.2, bias=-0.2 * math.log(2.0 * LOG_GAIN)
+            )
+            nc.sync.dma_start(out=out[blk(i), :], in_=result[i][:])

@@ -21,6 +21,7 @@ AX = mybir.AxisListType
 P = 128
 PACK = 4
 NB = 4
+EARLY = 2
 LOG_GAIN = 2.0 ** 12
 LOG_FLOOR = 2.0 ** -64
 
@@ -50,79 +51,81 @@ def tile_picked_yzinb_sq_p_kernel(
         e_word_table = one("e_word_table", [P, T], U32)
         x_word_table = one("x_word_table", [P, T], U32)
         theta_table = one("theta_table", [P, T], F32)
-        h_raw = tiles("h_raw", [P, PACK, 2 * P], F32, 2)
+        stage = one("stage", [P, 2, PACK, 2 * P], F32)
+        h_raw = [stage[:, 1], stage[:, 0]]
         cnt_sb = tiles("cnt_sb", [P, 2, S], F32, 2)
         zero_sb = tiles("zero_sb", [P, 2, S], F32, 2)
         lib_sb = one("lib_sb", [P, NB], F32)
         ident = one("ident", [P, P], F32)
 
-        def load_scales(table, scales):
-            for q in range(4):
+        def load_scales(queue, table, scales, quadrants):
+            for q in quadrants:
                 rows = scales[0, 4 * q : 4 * q + 4, :].bitcast(I32)
-                nc.sync.dma_start(
-                    out=table[32 * q : 32 * q + 32, :].bitcast(I32),
-                    in_=rows.partition_broadcast(8),
-                )
+                queue.dma_start(out=table[32 * q : 32 * q + 4, :].bitcast(I32), in_=rows)
 
         def load_words(table, words):
             nc.sync.dma_start(out=table[:].bitcast(I32), in_=words[0].rearrange("p n t -> p (n t)").bitcast(I32))
 
         def load_h(half):
             cols = hT[:, half * 2 * P : (half + 1) * 2 * P]
-            nc.sync.dma_start(out=h_raw[half][:], in_=cols.rearrange("(p t) c -> p t c", t=PACK))
+            nc.sync.dma_start(out=h_raw[half], in_=cols.rearrange("(p t) c -> p t c", t=PACK))
 
         def load_rows(dst, src, half):
             rows = src[half * 2 * P : (half + 1) * 2 * P, :]
             nc.sync.dma_start(out=dst[half][:], in_=rows.rearrange("(i p) g -> p i g", p=P))
 
-        nc.gpsimd.memset(theta_table[:], 0.0)
-        nc.scalar.dma_start(out=theta_table[0:1, :], in_=theta[0:1, :])
+        nc.vector.memset(e_scale_table[:].bitcast(I32), 0)
+        nc.vector.memset(x_scale_table[:].bitcast(I32), 0)
+        nc.vector.memset(theta_table[:], 0.0)
+        load_scales(nc.gpsimd, x_scale_table, x_scales, range(3))
+        nc.gpsimd.dma_start(out=theta_table[0:1, 0 : T // 2], in_=theta[0:1, 0 : T // 2])
         make_identity(nc, ident[:])
 
         nc.sync.dma_start(offsets[:], offs)
-        load_scales(e_scale_table, e_scales)
+        load_scales(nc.scalar, e_scale_table, e_scales, range(4))
         load_h(0)
         load_words(e_word_table, e_words)
-        load_scales(x_scale_table, x_scales)
         load_h(1)
+        load_scales(nc.sync, x_scale_table, x_scales, [3])
         load_words(x_word_table, x_words)
-        for half in range(2):
-            load_rows(zero_sb, zero, half)
-            load_rows(cnt_sb, cnt, half)
+        nc.sync.dma_start(out=theta_table[0:1, T // 2 : T], in_=theta[0:1, T // 2 : T])
         with nc.allow_non_contiguous_dma(reason="one library size a partition"):
             nc.sync.dma_start(out=lib_sb[:], in_=lib.rearrange("(i p) o -> p (i o)", p=P))
+        for half in range(2):
+            load_rows(zero_sb, zero, half)
+        for half in range(2):
+            load_rows(cnt_sb, cnt, half)
 
         def gather(name, table, dtype):
             picked = one(name, [P, S], dtype)
             nc.vector.tensor_copy(picked[:], table[:].indirect(offsets[:]))
             return picked
 
-        h_bf = tiles("h_bf", [P, P, PACK], BF16)
-        h_codes = tiles("h_codes", [P, P], U32)
-        h_scales = tiles("h_scales", [P, P], U8)
+        h_bf = tiles("h_bf", [P, 2 * P, PACK], BF16, 2)
+        h_codes = tiles("h_codes", [P, 2 * P], U32, 2)
+        h_scales = tiles("h_scales", [P, 2 * P], U8, 2)
 
-        def interleave(i):
-            src = h_raw[i // 2][:, :, blk(i % 2)]
+        def interleave(half):
             nc.scalar.activation(
-                out=h_bf[i][:].rearrange("p (c n) t -> p c t n", n=4),
-                in_=src.rearrange("p t (c n) -> p c t n", n=4),
+                out=h_bf[half][:].rearrange("p (c n) t -> p c t n", n=4),
+                in_=h_raw[half].rearrange("p t (c n) -> p c t n", n=4),
                 func=ACT.Copy,
             )
 
-        def quantize(i):
+        def quantize(half):
             nc.vector.quantize_mx(
-                out=h_codes[i][:].bitcast(FP8X4),
-                scales=h_scales[i][:],
-                in_=h_bf[i][:].rearrange("p c t -> p (c t)"),
+                out=h_codes[half][:].bitcast(FP8X4),
+                scales=h_scales[half][:],
+                in_=h_bf[half][:].rearrange("p c t -> p (c t)"),
             )
 
-        def product(bank, i, codes, scales):
+        def product(dst, rows, row_scales, cols, col_scales):
             nc.tensor.matmul_mx(
-                out=bank[:],
-                lhsT=h_codes[i][:].bitcast(FP8X4),
-                lhsT_scale=h_scales[i][:],
-                rhs=codes[:].bitcast(FP8X4),
-                rhs_scale=scales[:],
+                out=dst,
+                lhsT=rows.bitcast(FP8X4),
+                lhsT_scale=row_scales,
+                rhs=cols.bitcast(FP8X4),
+                rhs_scale=col_scales,
                 start=True,
                 stop=True,
             )
@@ -130,106 +133,131 @@ def tile_picked_yzinb_sq_p_kernel(
         def turn(dst, src, start=True, stop=True):
             nc.tensor.matmul(dst, src, ident[:], start=start, stop=stop, is_transpose=True)
 
-        for i in range(NB):
-            interleave(i)
+        for half in range(2):
+            interleave(half)
         e_scale = gather("e_scale", e_scale_table, U8)
-        theta_row = gather("theta_row", theta_table, F32)
         quantize(0)
-        quantize(1)
         e_code = gather("e_code", e_word_table, U32)
         x_scale = gather("x_scale", x_scale_table, U8)
-        quantize(2)
-        quantize(3)
+        quantize(1)
         x_code = gather("x_code", x_word_table, U32)
+        theta_row = gather("theta_row", theta_table, F32)
 
-        th = one("th", [P, NB], F32)
-        inv_th = one("inv_th", [P, NB], F32)
-        eps_th = one("eps_th", [P, NB], F32)
+        for half in range(2):
+            for pair in range(2):
+                bank = bank_b[2 * half + pair]
+                for n in range(2):
+                    genes = blk(2 * pair + n)
+                    dst = bank[:, n * 2 * P : (n + 1) * 2 * P]
+                    product(dst, e_code[:, genes], e_scale[:, genes], h_codes[half][:], h_scales[half][:])
+                nc.scalar.activation(
+                    out=stage[:, half, 2 * pair : 2 * pair + 2, :],
+                    in_=bank[:].rearrange("p (n c) -> p n c", n=2),
+                    func=ACT.Tanh,
+                    scale=0.5,
+                )
+
+        neg_th = one("neg_th", [P, NB], F32)
         for j in range(NB):
-            turn(bank_a[3][:, blk(j)], theta_row[:, blk(j)])
-        nc.vector.tensor_copy(th[:], bank_a[3][:, 0:S:P])
-        nc.vector.reciprocal(inv_th[:], th[:])
-        nc.vector.tensor_scalar(eps_th[:], inv_th[:], 0.001, None, ALU.mult)
-
-        tanh_half = one("tanh_half", [P, NB, S], F32)
-        for i in range(NB):
-            product(bank_b[i], i, e_code, e_scale)
-            nc.scalar.activation(out=tanh_half[:, i, :], in_=bank_b[i][:], func=ACT.Tanh, scale=0.5)
+            turn(bank_b[0][:, blk(j)], theta_row[:, blk(j)])
+        nc.scalar.activation(out=neg_th[:], in_=bank_b[0][:, 0:S:P], func=ACT.Copy, scale=-1.0)
 
         neg_max = one("neg_max", [P, NB], F32)
         total = one("total", [P, NB], F32)
         inv_total = one("inv_total", [P, NB], F32)
-        ex = tiles("ex", [P, S], F32)
+        ex_all = sb.tile([P, NB, S], F32, name="ex_all", tag="ex_then_gates", align_bytes=64)
+        ex = [ex_all[:, i, :] for i in range(NB)]
         mu = tiles("mu", [P, S], F32)
         for i in range(NB):
-            product(bank_a[i], i, x_code, x_scale)
+            product(
+                bank_a[i][:], h_codes[i // 2][:, blk(i % 2)], h_scales[i // 2][:, blk(i % 2)], x_code[:], x_scale[:]
+            )
             nc.vector.tensor_reduce(neg_max[:, i : i + 1], bank_a[i][:], AX.X, ALU.max, negate=True)
             nc.scalar.activation(
-                out=ex[i][:], in_=bank_a[i][:], func=ACT.Exp, bias=neg_max[:, i : i + 1], accum_out=total[:, i : i + 1]
+                out=ex[i], in_=bank_a[i][:], func=ACT.Exp, bias=neg_max[:, i : i + 1], accum_out=total[:, i : i + 1]
             )
         for i in range(NB):
             nc.vector.reciprocal(inv_total[:, i : i + 1], total[:, i : i + 1])
             nc.vector.tensor_scalar(
-                mu[i][:], ex[i][:], inv_total[:, i : i + 1], lib_sb[:, i : i + 1], ALU.mult, ALU.mult
+                mu[i][:], ex[i], inv_total[:, i : i + 1], lib_sb[:, i : i + 1], ALU.mult, ALU.mult
             )
             for j in range(NB):
-                turn(bank_b[j][:, blk(i)], mu[i][:, blk(j)])
+                turn(bank_a[j][:, blk(i)], mu[i][:, blk(j)])
 
-        neg_cz = tiles("neg_cz", [P, S], F32)
-        for i in range(NB):
-            nc.vector.scalar_tensor_tensor(
-                neg_cz[i][:], zero_sb[i // 2][:, i % 2, :], 1.0, cnt_sb[i // 2][:, i % 2, :], ALU.subtract, ALU.mult
-            )
-            for j in range(NB):
-                turn(bank_a[j][:, blk(i)], neg_cz[i][:, blk(j)])
+        neg_inv_th = one("neg_inv_th", [P, NB], F32)
+        inv_th = one("inv_th", [P, NB], F32)
+        eps_th = one("eps_th", [P, NB], F32)
+        nc.vector.reciprocal(neg_inv_th[:], neg_th[:])
+        nc.vector.tensor_scalar(inv_th[:], neg_inv_th[:], -1.0, None, ALU.mult)
+        nc.vector.tensor_scalar(eps_th[:], neg_inv_th[:], -0.001, None, ALU.mult)
+
+        def turn_rows(banks, rows, j):
+            for i in range(NB):
+                turn(banks[j][:, blk(i)], rows[i // 2][:, i % 2, blk(j)])
 
         log_m = tiles("log_m", [P, V], F32)
         log_l = tiles("log_l", [P, V], F32)
-        term_m = tiles("term_m", [P, V], F32)
-        term_l = tiles("term_l", [P, V], F32)
+        log_ratio = tiles("log_ratio", [P, V], F32)
         for j in range(NB):
             col = slice(j, j + 1)
+            nc.scalar.activation(out=log_l[j][:], in_=bank_a[j][:], func=ACT.Ln, scale=inv_th[:, col], bias=1.0)
             nc.scalar.activation(
-                out=log_m[j][:], in_=bank_b[j][:], func=ACT.Ln, scale=inv_th[:, col], bias=eps_th[:, col]
+                out=log_m[j][:], in_=bank_a[j][:], func=ACT.Ln, scale=inv_th[:, col], bias=eps_th[:, col]
             )
-            nc.scalar.activation(out=log_l[j][:], in_=bank_b[j][:], func=ACT.Ln, scale=inv_th[:, col], bias=1.0)
-            nc.vector.scalar_tensor_tensor(term_m[j][:], bank_a[j][:], -1.0, log_m[j][:], ALU.mult, ALU.mult)
-            nc.vector.scalar_tensor_tensor(
-                term_l[j][:], bank_a[j][:], th[:, col], log_l[j][:], ALU.subtract, ALU.mult
-            )
-            for i in range(NB):
-                turn(bank_b[j][:, blk(i)], term_m[j][:, blk(i)], start=(i == 0), stop=False)
-            for i in range(NB):
-                turn(bank_b[j][:, blk(i)], term_l[j][:, blk(i)], start=False, stop=(i == NB - 1))
+            nc.gpsimd.tensor_tensor(log_ratio[j][:], log_l[j][:], log_m[j][:], ALU.subtract)
 
-        keep = one("keep", [P, NB, S], F32)
-        drop = tiles("drop", [P, S], F32)
-        for i in range(NB):
-            z = zero_sb[i // 2][:, i % 2, :]
-            nc.vector.scalar_tensor_tensor(keep[:, i, :], z, -2e-4, tanh_half[:, i, :], ALU.mult, ALU.subtract)
-        for i in range(NB):
-            z = zero_sb[i // 2][:, i % 2, :]
-            nc.vector.scalar_tensor_tensor(drop[i][:], tanh_half[:, i, :], 1.0, z, ALU.add, ALU.mult)
-            for j in range(NB):
-                turn(bank_a[i][:, blk(j)], drop[i][:, blk(j)], start=(j == 0), stop=False)
+        def halves(t):
+            return t.rearrange("p (h c) -> p h c", h=2)
 
-        nb = tiles("nb", [P, NB, P], F32)
-        kept = tiles("kept", [P, NB, P], F32)
+        gates = sb.tile([P, 2, NB, V], F32, name="gates", tag="ex_then_gates", align_bytes=64)
+        keep = [gates[:, 0, j, :] for j in range(NB)]
+        drop = [gates[:, 1, j, :] for j in range(NB)]
+        zero_t = [bank_b[(j + 1) % NB] for j in range(NB)]
         for j in range(NB):
-            nc.scalar.activation(out=nb[j][:].rearrange("p i c -> p (i c)"), in_=bank_b[j][:], func=ACT.Exp)
-            nc.vector.scalar_tensor_tensor(kept[j][:], keep[:, :, blk(j)], 1.0002, nb[j][:], ALU.add, ALU.mult)
-            for i in range(NB):
-                turn(bank_a[i][:, blk(j)], kept[j][:, i, :], start=False, stop=(j == NB - 1))
+            turn_rows(zero_t, zero_sb, j)
+            tanh_half = stage[:, :, j, :]
+            z = halves(zero_t[j][:])
+            nc.vector.scalar_tensor_tensor(halves(keep[j]), z, -2e-4, tanh_half, ALU.mult, ALU.subtract)
+            nc.vector.scalar_tensor_tensor(halves(drop[j]), tanh_half, 1.0, z, ALU.add, ALU.mult)
 
-        log_w = tiles("log_w", [P, S], F32)
-        for i in range(NB):
-            nc.scalar.activation(out=log_w[i][:], in_=bank_a[i][:], func=ACT.Ln, scale=LOG_GAIN, bias=LOG_FLOOR)
-            for j in range(NB):
-                turn(bank_b[i][:, blk(j)], log_w[i][:, blk(j)])
+        counted = tiles("counted", [P, V], F32)
+        for j in range(NB):
+            turn_rows(bank_a, cnt_sb, j)
+            nc.vector.tensor_tensor(counted[j][:], bank_a[j][:], log_ratio[j][:], ALU.mult)
+
+        count_term = tiles("count_term", [P, V], F32)
+
+        def add_count_term(j):
+            nc.vector.scalar_tensor_tensor(count_term[j][:], zero_t[j][:], 1.0, counted[j][:], ALU.subtract, ALU.mult)
+            for i in range(NB):
+                turn(bank_a[i][:, blk(j)], count_term[j][:, blk(i)], start=(j == 0), stop=False)
+
+        for j in range(EARLY):
+            add_count_term(j)
+
+        nb_zero = tiles("nb_zero", [P, V], F32)
+        kept = tiles("kept", [P, V], F32)
+        mix = tiles("mix", [P, V], F32)
+        for j in range(NB):
+            nc.scalar.activation(out=nb_zero[j][:], in_=log_l[j][:], func=ACT.Exp, scale=neg_th[:, j : j + 1])
+        for j in range(NB + 1):
+            if j < NB:
+                nc.vector.scalar_tensor_tensor(kept[j][:], keep[j], 1.0002, nb_zero[j][:], ALU.add, ALU.mult)
+            if j > 0:
+                nc.vector.tensor_tensor(mix[j - 1][:], kept[j - 1][:], drop[j - 1], ALU.add)
+
+        log_w = tiles("log_w", [P, V], F32)
+        for j in range(NB):
+            nc.scalar.activation(out=log_w[j][:], in_=mix[j][:], func=ACT.Ln, scale=LOG_GAIN, bias=LOG_FLOOR)
+        for j in range(NB):
+            if j >= EARLY:
+                add_count_term(j)
+            for i in range(NB):
+                turn(bank_a[i][:, blk(j)], log_w[j][:, blk(i)], start=False, stop=(j == NB - 1))
 
         result = tiles("result", [P, S], F32)
         for i in range(NB):
             nc.scalar.activation(
-                out=result[i][:], in_=bank_b[i][:], func=ACT.Tanh, scale=0.2, bias=-0.2 * math.log(2.0 * LOG_GAIN)
+                out=result[i][:], in_=bank_a[i][:], func=ACT.Tanh, scale=0.2, bias=-0.2 * math.log(2.0 * LOG_GAIN)
             )
             nc.sync.dma_start(out=out[blk(i), :], in_=result[i][:])

@@ -21,7 +21,7 @@ AX = mybir.AxisListType
 P = 128
 PACK = 4
 NB = 4
-EARLY = 2
+EARLY = 3
 LOG_GAIN = 2.0 ** 12
 LOG_FLOOR = 2.0 ** -64
 
@@ -46,8 +46,8 @@ def tile_picked_yzinb_sq_p_kernel(
         bank_a = [ps.tile([P, S], F32, name="bank_a" + str(b)) for b in range(NB)]
         bank_b = [ps.tile([P, S], F32, name="bank_b" + str(b)) for b in range(NB)]
 
-        e_scale_table = one("e_scale_table", [P, T], U8)
-        x_scale_table = one("x_scale_table", [P, T], U8)
+        e_scale_table = sb.tile([P, T], U8, name="e_scale_table", tag="scale_bytes0", align_bytes=64)
+        x_scale_table = sb.tile([P, T], U8, name="x_scale_table", tag="scale_bytes1", align_bytes=64)
         e_word_table = one("e_word_table", [P, T], U32)
         x_word_table = one("x_word_table", [P, T], U32)
         theta_table = one("theta_table", [P, T], F32)
@@ -58,10 +58,10 @@ def tile_picked_yzinb_sq_p_kernel(
         lib_sb = one("lib_sb", [P, NB], F32)
         ident = one("ident", [P, P], F32)
 
-        def load_scales(queue, table, scales, quadrants):
-            for q in quadrants:
+        def load_scales(table, scales):
+            for q in range(4):
                 rows = scales[0, 4 * q : 4 * q + 4, :].bitcast(I32)
-                queue.dma_start(out=table[32 * q : 32 * q + 4, :].bitcast(I32), in_=rows)
+                nc.sync.dma_start(out=table[32 * q : 32 * q + 4, :].bitcast(I32), in_=rows)
 
         def load_words(table, words):
             nc.sync.dma_start(out=table[:].bitcast(I32), in_=words[0].rearrange("p n t -> p (n t)").bitcast(I32))
@@ -77,16 +77,15 @@ def tile_picked_yzinb_sq_p_kernel(
         nc.vector.memset(e_scale_table[:].bitcast(I32), 0)
         nc.vector.memset(x_scale_table[:].bitcast(I32), 0)
         nc.vector.memset(theta_table[:], 0.0)
-        load_scales(nc.gpsimd, x_scale_table, x_scales, range(3))
-        nc.gpsimd.dma_start(out=theta_table[0:1, 0 : T // 2], in_=theta[0:1, 0 : T // 2])
         make_identity(nc, ident[:])
 
         nc.sync.dma_start(offsets[:], offs)
-        load_scales(nc.scalar, e_scale_table, e_scales, range(4))
         load_h(0)
+        load_scales(e_scale_table, e_scales)
         load_words(e_word_table, e_words)
         load_h(1)
-        load_scales(nc.sync, x_scale_table, x_scales, [3])
+        load_scales(x_scale_table, x_scales)
+        nc.sync.dma_start(out=theta_table[0:1, 0 : T // 2], in_=theta[0:1, 0 : T // 2])
         load_words(x_word_table, x_words)
         nc.sync.dma_start(out=theta_table[0:1, T // 2 : T], in_=theta[0:1, T // 2 : T])
         with nc.allow_non_contiguous_dma(reason="one library size a partition"):
@@ -103,7 +102,7 @@ def tile_picked_yzinb_sq_p_kernel(
 
         h_bf = tiles("h_bf", [P, 2 * P, PACK], BF16, 2)
         h_codes = tiles("h_codes", [P, 2 * P], U32, 2)
-        h_scales = tiles("h_scales", [P, 2 * P], U8, 2)
+        h_scales = [None, None]
 
         def interleave(half):
             nc.scalar.activation(
@@ -113,6 +112,9 @@ def tile_picked_yzinb_sq_p_kernel(
             )
 
         def quantize(half):
+            h_scales[half] = sb.tile(
+                [P, 2 * P], U8, name="h_scales" + str(half), tag="scale_bytes" + str(half), align_bytes=64
+            )
             nc.vector.quantize_mx(
                 out=h_codes[half][:].bitcast(FP8X4),
                 scales=h_scales[half][:],
@@ -204,14 +206,17 @@ def tile_picked_yzinb_sq_p_kernel(
             nc.scalar.activation(
                 out=log_m[j][:], in_=bank_a[j][:], func=ACT.Ln, scale=inv_th[:, col], bias=eps_th[:, col]
             )
-            nc.gpsimd.tensor_tensor(log_ratio[j][:], log_l[j][:], log_m[j][:], ALU.subtract)
+            nc.gpsimd.tensor_tensor(log_ratio[j][:], log_m[j][:], log_l[j][:], ALU.subtract)
 
         def halves(t):
             return t.rearrange("p (h c) -> p h c", h=2)
 
-        gates = sb.tile([P, 2, NB, V], F32, name="gates", tag="ex_then_gates", align_bytes=64)
+        gates = sb.tile([P, 3, NB, V], F32, name="gates", tag="ex_then_gates", align_bytes=64)
         keep = [gates[:, 0, j, :] for j in range(NB)]
         drop = [gates[:, 1, j, :] for j in range(NB)]
+        veto = gates[:, 2]
+        for half in range(2):
+            nc.vector.tensor_scalar(veto[:, 2 * half : 2 * half + 2, :], zero_sb[half][:], -1e30, None, ALU.mult)
         zero_t = [bank_b[(j + 1) % NB] for j in range(NB)]
         for j in range(NB):
             turn_rows(zero_t, zero_sb, j)
@@ -220,17 +225,17 @@ def tile_picked_yzinb_sq_p_kernel(
             nc.vector.scalar_tensor_tensor(halves(keep[j]), z, -2e-4, tanh_half, ALU.mult, ALU.subtract)
             nc.vector.scalar_tensor_tensor(halves(drop[j]), tanh_half, 1.0, z, ALU.add, ALU.mult)
 
-        counted = tiles("counted", [P, V], F32)
-        for j in range(NB):
-            turn_rows(bank_a, cnt_sb, j)
-            nc.vector.tensor_tensor(counted[j][:], bank_a[j][:], log_ratio[j][:], ALU.mult)
-
         count_term = tiles("count_term", [P, V], F32)
+        for j in range(NB):
+            for i in range(NB):
+                turn(bank_a[j][:, blk(i)], cnt_sb[i // 2][:, i % 2, blk(j)], start=(i == 0), stop=False)
+            for i in range(NB):
+                turn(bank_a[j][:, blk(i)], veto[:, i, blk(j)], start=False, stop=(i == NB - 1))
+            nc.vector.scalar_tensor_tensor(count_term[j][:], bank_a[j][:], 0.0, log_ratio[j][:], ALU.max, ALU.mult)
 
         def add_count_term(j):
-            nc.vector.scalar_tensor_tensor(count_term[j][:], zero_t[j][:], 1.0, counted[j][:], ALU.subtract, ALU.mult)
             for i in range(NB):
-                turn(bank_a[i][:, blk(j)], count_term[j][:, blk(i)], start=(j == 0), stop=False)
+                turn(bank_a[i][:, blk(j)], count_term[j][:, blk(i)], start=(j == 0), stop=(j == NB - 1))
 
         for j in range(EARLY):
             add_count_term(j)
@@ -250,14 +255,21 @@ def tile_picked_yzinb_sq_p_kernel(
         for j in range(NB):
             nc.scalar.activation(out=log_w[j][:], in_=mix[j][:], func=ACT.Ln, scale=LOG_GAIN, bias=LOG_FLOOR)
         for j in range(NB):
+            for i in range(NB):
+                turn(bank_a[i][:, blk(j)], log_w[j][:, blk(i)], start=False, stop=False)
             if j >= EARLY:
                 add_count_term(j)
-            for i in range(NB):
-                turn(bank_a[i][:, blk(j)], log_w[j][:, blk(i)], start=False, stop=(j == NB - 1))
 
         result = tiles("result", [P, S], F32)
         for i in range(NB):
-            nc.scalar.activation(
-                out=result[i][:], in_=bank_a[i][:], func=ACT.Tanh, scale=0.2, bias=-0.2 * math.log(2.0 * LOG_GAIN)
-            )
-            nc.sync.dma_start(out=out[blk(i), :], in_=result[i][:])
+            pieces = 2 if i == NB - 1 else 1
+            for n in range(pieces):
+                genes = slice(n * S // pieces, (n + 1) * S // pieces)
+                nc.scalar.activation(
+                    out=result[i][:, genes],
+                    in_=bank_a[i][:, genes],
+                    func=ACT.Tanh,
+                    scale=0.2,
+                    bias=-0.2 * math.log(2.0 * LOG_GAIN),
+                )
+                nc.sync.dma_start(out=out[blk(i), genes], in_=result[i][:, genes])

import math
from contextlib import ExitStack

import concourse.mybir as mybir
from concourse.masks import make_identity

K, T, S, V = 512, 1024, 512, 512
FLOPS = 2 * 2 * K * V * S

F32 = mybir.dt.float32
BF16 = mybir.dt.bfloat16
I32 = mybir.dt.int32
U32 = mybir.dt.uint32
U16 = mybir.dt.uint16
U8 = mybir.dt.uint8
FP8X4 = mybir.dt.float8_e4m3fn_x4
ALU = mybir.AluOpType
ACT = mybir.ActivationFunctionType
AX = mybir.AxisListType

P = 128
PACK = 4
NB = 4
EARLY = 3
LOG_GAIN = 2.0 ** 12
LOG_FLOOR = 2.0 ** -64


def tile_picked_yzinb_sq_p_kernel(
    tc, x_words, x_scales, hT, e_words, e_scales, lib, theta, cnt, zero, offs, out
):
    nc = tc.nc
    blk = lambda b: slice(b * P, (b + 1) * P)

    with ExitStack() as ctx:
        sb = ctx.enter_context(tc.tile_pool(name="sb", bufs=1))
        ps = ctx.enter_context(tc.psum_pool(name="ps", bufs=1))

        def tiles(name, shape, dtype, n=NB):
            return [sb.tile(shape, dtype, name=name + str(b), align_bytes=64) for b in range(n)]

        def one(name, shape, dtype):
            return sb.tile(shape, dtype, name=name, align_bytes=64)

        offsets = sb.tile([P, S // 16], U16, name="offsets")
        bank_a = [ps.tile([P, S], F32, name="bank_a" + str(b)) for b in range(NB)]
        bank_b = [ps.tile([P, S], F32, name="bank_b" + str(b)) for b in range(NB)]

        e_scale_table = sb.tile([P, T], U8, name="e_scale_table", tag="scale_bytes0", align_bytes=64)
        x_scale_table = sb.tile([P, T], U8, name="x_scale_table", tag="scale_bytes1", align_bytes=64)
        e_word_table = one("e_word_table", [P, T], U32)
        x_word_table = one("x_word_table", [P, T], U32)
        theta_table = one("theta_table", [P, T], F32)
        stage = one("stage", [P, 2, PACK, 2 * P], F32)
        h_raw = [stage[:, 1], stage[:, 0]]
        cnt_sb = tiles("cnt_sb", [P, 2, S], F32, 2)
        zero_sb = tiles("zero_sb", [P, 2, S], F32, 2)
        lib_sb = one("lib_sb", [P, NB], F32)
        ident = one("ident", [P, P], F32)

        def load_scales(table, scales):
            for q in range(4):
                rows = scales[0, 4 * q : 4 * q + 4, :].bitcast(I32)
                nc.sync.dma_start(out=table[32 * q : 32 * q + 4, :].bitcast(I32), in_=rows)

        def load_words(table, words):
            nc.sync.dma_start(out=table[:].bitcast(I32), in_=words[0].rearrange("p n t -> p (n t)").bitcast(I32))

        def load_h(half):
            cols = hT[:, half * 2 * P : (half + 1) * 2 * P]
            nc.sync.dma_start(out=h_raw[half], in_=cols.rearrange("(p t) c -> p t c", t=PACK))

        def load_rows(dst, src, half):
            rows = src[half * 2 * P : (half + 1) * 2 * P, :]
            nc.sync.dma_start(out=dst[half][:], in_=rows.rearrange("(i p) g -> p i g", p=P))

        nc.vector.memset(e_scale_table[:].bitcast(I32), 0)
        nc.vector.memset(x_scale_table[:].bitcast(I32), 0)
        nc.vector.memset(theta_table[:], 0.0)
        make_identity(nc, ident[:])

        nc.sync.dma_start(offsets[:], offs)
        load_h(0)
        load_scales(e_scale_table, e_scales)
        load_words(e_word_table, e_words)
        load_h(1)
        load_scales(x_scale_table, x_scales)
        nc.sync.dma_start(out=theta_table[0:1, 0 : T // 2], in_=theta[0:1, 0 : T // 2])
        load_words(x_word_table, x_words)
        nc.sync.dma_start(out=theta_table[0:1, T // 2 : T], in_=theta[0:1, T // 2 : T])
        with nc.allow_non_contiguous_dma(reason="one library size a partition"):
            nc.sync.dma_start(out=lib_sb[:], in_=lib.rearrange("(i p) o -> p (i o)", p=P))
        for half in range(2):
            load_rows(zero_sb, zero, half)
        for half in range(2):
            load_rows(cnt_sb, cnt, half)

        def gather(name, table, dtype):
            picked = one(name, [P, S], dtype)
            nc.vector.tensor_copy(picked[:], table[:].indirect(offsets[:]))
            return picked

        h_bf = tiles("h_bf", [P, 2 * P, PACK], BF16, 2)
        h_codes = tiles("h_codes", [P, 2 * P], U32, 2)
        h_scales = [None, None]

        def interleave(half):
            nc.scalar.activation(
                out=h_bf[half][:].rearrange("p (c n) t -> p c t n", n=4),
                in_=h_raw[half].rearrange("p t (c n) -> p c t n", n=4),
                func=ACT.Copy,
            )

        def quantize(half):
            h_scales[half] = sb.tile(
                [P, 2 * P], U8, name="h_scales" + str(half), tag="scale_bytes" + str(half), align_bytes=64
            )
            nc.vector.quantize_mx(
                out=h_codes[half][:].bitcast(FP8X4),
                scales=h_scales[half][:],
                in_=h_bf[half][:].rearrange("p c t -> p (c t)"),
            )

        def product(dst, rows, row_scales, cols, col_scales):
            nc.tensor.matmul_mx(
                out=dst,
                lhsT=rows.bitcast(FP8X4),
                lhsT_scale=row_scales,
                rhs=cols.bitcast(FP8X4),
                rhs_scale=col_scales,
                start=True,
                stop=True,
            )

        def turn(dst, src, start=True, stop=True):
            nc.tensor.matmul(dst, src, ident[:], start=start, stop=stop, is_transpose=True)

        for half in range(2):
            interleave(half)
        e_scale = gather("e_scale", e_scale_table, U8)
        quantize(0)
        e_code = gather("e_code", e_word_table, U32)
        x_scale = gather("x_scale", x_scale_table, U8)
        quantize(1)
        x_code = gather("x_code", x_word_table, U32)
        theta_row = gather("theta_row", theta_table, F32)

        for half in range(2):
            for pair in range(2):
                bank = bank_b[2 * half + pair]
                for n in range(2):
                    genes = blk(2 * pair + n)
                    dst = bank[:, n * 2 * P : (n + 1) * 2 * P]
                    product(dst, e_code[:, genes], e_scale[:, genes], h_codes[half][:], h_scales[half][:])
                nc.scalar.activation(
                    out=stage[:, half, 2 * pair : 2 * pair + 2, :],
                    in_=bank[:].rearrange("p (n c) -> p n c", n=2),
                    func=ACT.Tanh,
                    scale=0.5,
                )

        neg_th = one("neg_th", [P, NB], F32)
        for j in range(NB):
            turn(bank_b[0][:, blk(j)], theta_row[:, blk(j)])
        nc.scalar.activation(out=neg_th[:], in_=bank_b[0][:, 0:S:P], func=ACT.Copy, scale=-1.0)

        neg_max = one("neg_max", [P, NB], F32)
        total = one("total", [P, NB], F32)
        inv_total = one("inv_total", [P, NB], F32)
        ex_all = sb.tile([P, NB, S], F32, name="ex_all", tag="ex_then_gates", align_bytes=64)
        ex = [ex_all[:, i, :] for i in range(NB)]
        mu = tiles("mu", [P, S], F32)
        for i in range(NB):
            product(
                bank_a[i][:], h_codes[i // 2][:, blk(i % 2)], h_scales[i // 2][:, blk(i % 2)], x_code[:], x_scale[:]
            )
            nc.vector.tensor_reduce(neg_max[:, i : i + 1], bank_a[i][:], AX.X, ALU.max, negate=True)
            nc.scalar.activation(
                out=ex[i], in_=bank_a[i][:], func=ACT.Exp, bias=neg_max[:, i : i + 1], accum_out=total[:, i : i + 1]
            )
        for i in range(NB):
            nc.vector.reciprocal(inv_total[:, i : i + 1], total[:, i : i + 1])
            nc.vector.tensor_scalar(
                mu[i][:], ex[i], inv_total[:, i : i + 1], lib_sb[:, i : i + 1], ALU.mult, ALU.mult
            )
            for j in range(NB):
                turn(bank_a[j][:, blk(i)], mu[i][:, blk(j)])

        neg_inv_th = one("neg_inv_th", [P, NB], F32)
        inv_th = one("inv_th", [P, NB], F32)
        eps_th = one("eps_th", [P, NB], F32)
        nc.vector.reciprocal(neg_inv_th[:], neg_th[:])
        nc.vector.tensor_scalar(inv_th[:], neg_inv_th[:], -1.0, None, ALU.mult)
        nc.vector.tensor_scalar(eps_th[:], neg_inv_th[:], -0.001, None, ALU.mult)

        def turn_rows(banks, rows, j):
            for i in range(NB):
                turn(banks[j][:, blk(i)], rows[i // 2][:, i % 2, blk(j)])

        log_m = tiles("log_m", [P, V], F32)
        log_l = tiles("log_l", [P, V], F32)
        log_ratio = tiles("log_ratio", [P, V], F32)
        for j in range(NB):
            col = slice(j, j + 1)
            nc.scalar.activation(out=log_l[j][:], in_=bank_a[j][:], func=ACT.Ln, scale=inv_th[:, col], bias=1.0)
            nc.scalar.activation(
                out=log_m[j][:], in_=bank_a[j][:], func=ACT.Ln, scale=inv_th[:, col], bias=eps_th[:, col]
            )
            nc.gpsimd.tensor_tensor(log_ratio[j][:], log_m[j][:], log_l[j][:], ALU.subtract)

        def halves(t):
            return t.rearrange("p (h c) -> p h c", h=2)

        gates = sb.tile([P, 3, NB, V], F32, name="gates", tag="ex_then_gates", align_bytes=64)
        keep = [gates[:, 0, j, :] for j in range(NB)]
        drop = [gates[:, 1, j, :] for j in range(NB)]
        veto = gates[:, 2]
        for half in range(2):
            nc.vector.tensor_scalar(veto[:, 2 * half : 2 * half + 2, :], zero_sb[half][:], -1e30, None, ALU.mult)
        zero_t = [bank_b[(j + 1) % NB] for j in range(NB)]
        for j in range(NB):
            turn_rows(zero_t, zero_sb, j)
            tanh_half = stage[:, :, j, :]
            z = halves(zero_t[j][:])
            nc.vector.scalar_tensor_tensor(halves(keep[j]), z, -2e-4, tanh_half, ALU.mult, ALU.subtract)
            nc.vector.scalar_tensor_tensor(halves(drop[j]), tanh_half, 1.0, z, ALU.add, ALU.mult)

        count_term = tiles("count_term", [P, V], F32)
        for j in range(NB):
            for i in range(NB):
                turn(bank_a[j][:, blk(i)], cnt_sb[i // 2][:, i % 2, blk(j)], start=(i == 0), stop=False)
            for i in range(NB):
                turn(bank_a[j][:, blk(i)], veto[:, i, blk(j)], start=False, stop=(i == NB - 1))
            nc.vector.scalar_tensor_tensor(count_term[j][:], bank_a[j][:], 0.0, log_ratio[j][:], ALU.max, ALU.mult)

        def add_count_term(j):
            for i in range(NB):
                turn(bank_a[i][:, blk(j)], count_term[j][:, blk(i)], start=(j == 0), stop=(j == NB - 1))

        for j in range(EARLY):
            add_count_term(j)

        nb_zero = tiles("nb_zero", [P, V], F32)
        kept = tiles("kept", [P, V], F32)
        mix = tiles("mix", [P, V], F32)
        for j in range(NB):
            nc.scalar.activation(out=nb_zero[j][:], in_=log_l[j][:], func=ACT.Exp, scale=neg_th[:, j : j + 1])
        for j in range(NB + 1):
            if j < NB:
                nc.vector.scalar_tensor_tensor(kept[j][:], keep[j], 1.0002, nb_zero[j][:], ALU.add, ALU.mult)
            if j > 0:
                nc.vector.tensor_tensor(mix[j - 1][:], kept[j - 1][:], drop[j - 1], ALU.add)

        log_w = tiles("log_w", [P, V], F32)
        for j in range(NB):
            nc.scalar.activation(out=log_w[j][:], in_=mix[j][:], func=ACT.Ln, scale=LOG_GAIN, bias=LOG_FLOOR)
        for j in range(NB):
            for i in range(NB):
                turn(bank_a[i][:, blk(j)], log_w[j][:, blk(i)], start=False, stop=False)
            if j >= EARLY:
                add_count_term(j)

        result = tiles("result", [P, S], F32)
        for i in range(NB):
            pieces = 2 if i == NB - 1 else 1
            for n in range(pieces):
                genes = slice(n * S // pieces, (n + 1) * S // pieces)
                nc.scalar.activation(
                    out=result[i][:, genes],
                    in_=bank_a[i][:, genes],
                    func=ACT.Tanh,
                    scale=0.2,
                    bias=-0.2 * math.log(2.0 * LOG_GAIN),
                )
                nc.sync.dma_start(out=out[blk(i), genes], in_=result[i][:, genes])
